import numpy as np
import ml_dtypes


def mxq(x, axis, fmt="e4m3"):
    dtype, down = {"e4m3": (ml_dtypes.float8_e4m3fn, 7), "e5m2": (ml_dtypes.float8_e5m2, 14)}[fmt]
    v = np.moveaxis(np.asarray(x, np.float32).astype(ml_dtypes.bfloat16).astype(np.float64), axis, -1)
    blocks = v.reshape(v.shape[:-1] + (-1, 32))
    amax = np.abs(blocks).max(-1, keepdims=True)
    byte = np.maximum(np.where(amax > 0, np.frexp(amax)[1] - 1 + 127, 0) - down, 1)
    scale = np.exp2(byte - 127.0)
    codes = (blocks / scale).astype(np.float32).astype(dtype).astype(np.float64)
    return np.moveaxis((codes * scale).reshape(v.shape), -1, axis)


WIDE = False


def mx_kscale(k):
    if not WIDE:
        return np.ones(k)
    levels = np.array([10, -10, 5, -5, 0])
    if k % 512:
        return np.exp2(np.random.permutation(np.resize(levels, k // 32))).repeat(32)
    a = np.empty((k // 512, 16))
    for p in range(k // 512):
        a[p, :8] = np.random.permutation(np.resize(levels, 8))
        for g in range(8):
            far = levels[np.abs(levels - a[p, g]) >= 10]
            a[p, g + 8] = far[np.random.randint(len(far))]
    return np.exp2(a.ravel()).repeat(32)


BF16 = ml_dtypes.bfloat16


def bf(x):
    return np.asarray(x, np.float32).astype(BF16)


def f64(x):
    return np.asarray(x).astype(np.float64)


E2M1 = np.array([0.0, 0.5, 1.0, 1.5, 2.0, 3.0, 4.0, 6.0, -0.0, -0.5, -1.0, -1.5, -2.0, -3.0, -4.0, -6.0])


def pack_weight(w, fmt):
    k, n = w.shape
    w = f64(bf(w)).reshape(k // 32, 32, n)
    amax = np.abs(w).max(1)
    if fmt == "e4m3":
        byte = np.frexp(amax)[1] - 1 + 127 - 7
    else:
        mant, ex = np.frexp(amax / 6.0)
        byte = np.where(mant > 0.5, ex, ex - 1) + 127
    byte = np.clip(np.where(amax > 0, byte, 1), 1, 254)
    scaled = (w * np.exp2(127.0 - byte)[:, None, :]).reshape(k, n).astype(np.float32)
    by_word = np.ascontiguousarray(scaled.reshape(k // 512, 128, 4, n).transpose(0, 1, 3, 2))
    if fmt == "e4m3":
        words = by_word.astype(ml_dtypes.float8_e4m3fn).view(np.uint8)
    else:
        c = by_word.astype(ml_dtypes.float4_e2m1fn).view(np.uint8) & 0xF
        words = c[..., 0::2] | (c[..., 1::2] << 4)
    return np.ascontiguousarray(words), np.ascontiguousarray(byte.astype(np.uint8).reshape(k // 512, 16, n))


def unpack_weight(words, scales, fmt):
    g, p, n, _ = words.shape
    if fmt == "e4m3":
        vals = np.ascontiguousarray(words).view(ml_dtypes.float8_e4m3fn).astype(np.float64)
    else:
        nib = np.empty((g, p, n, 4), np.uint8)
        nib[..., 0::2] = words & 0xF
        nib[..., 1::2] = words >> 4
        vals = E2M1[nib]
    vals = vals * np.repeat(np.exp2(scales.astype(np.float64) - 127.0), 8, axis=1)[..., None]
    return vals.transpose(0, 1, 3, 2).reshape(g * 512, n)
def pack4(w):
    words, scales = pack_weight(w, "e2m1")
    return words.reshape(words.shape[0], 128, -1), scales


def unpack4(words, scales):
    return unpack_weight(words.reshape(words.shape[0], 128, -1, 2), scales, "e2m1")


G, P, K, N, D = 8, 512, 1024, 512, 512


def draw0():
    s = mx_kscale(K)
    t = mx_kscale(N)
    coef = np.random.standard_normal((G, K, N)) / np.sqrt(K) / s[:, None]
    bank = np.random.standard_normal((G, N, 2 * D)) / np.sqrt(N) / t[:, None]
    coef_words, coef_scales = pack4(coef.reshape(G * K, N))
    bank_words, bank_scales = pack4(bank.reshape(G * N, 2 * D))
    return {"past": bf(np.random.standard_normal((G, P, K)) * s),
            "now": bf(np.random.standard_normal((G, P, N))),
            "taper": bf((1 + 0.1 * np.random.standard_normal((G, N))) * t),
            "coef_words": coef_words, "coef_scales": coef_scales,
            "bank_words": bank_words, "bank_scales": bank_scales}


def core(past, now, taper, coef_words, coef_scales, bank_words, bank_scales):
    coef = unpack4(coef_words, coef_scales).reshape(G, K, N)
    bank = unpack4(bank_words, bank_scales).reshape(G, N, 2 * D)
    pred = mxq(f64(past), 2, "e4m3") @ coef
    e = (f64(now) - pred) * f64(taper)[:, None, :]
    y = mxq(e, 2, "e4m3") @ bank
    return np.sqrt(np.square(y[:, :, :D]) + np.square(y[:, :, D:]))


def e4m3fn_bytes(y):
    return np.clip(np.asarray(y, np.float64), -448.0, 448.0).astype(np.float32).astype(ml_dtypes.float8_e4m3fn).view(np.uint8)


def e4m3fn_values(b):
    return np.asarray(b, np.uint8).view(ml_dtypes.float8_e4m3fn).astype(np.float64)


def setup_inputs():
    d = draw0()
    x0 = np.asarray(d['past']).astype(np.float64)
    s = (np.max(np.abs(x0), axis=(0, 1), keepdims=True) / 448.0).astype(np.float32)
    out = {}
    for k, v in d.items():
        if k == 'past':
            out['past_bytes'] = e4m3fn_bytes(x0 / s.astype(np.float64))
            out['past_scale'] = s
        else:
            out[k] = v
    return out


def reference(past_bytes, past_scale, now, taper, coef_words, coef_scales, bank_words, bank_scales):
    return core(e4m3fn_values(past_bytes) * past_scale.astype(np.float64), now, taper, coef_words, coef_scales, bank_words, bank_scales)

@@ -1,0 +1,258 @@
+from contextlib import ExitStack
+
+import concourse.mybir as mybir
+from concourse.masks import make_identity
+
+BEAMS, PINGS, PAST, NOW, DOPPLER = 8, 512, 1024, 512, 512
+FLOPS = 2 * BEAMS * PINGS * (PAST * NOW + NOW * 2 * DOPPLER)
+
+P = 128
+UNITS = PINGS // P
+STEPS = BEAMS * UNITS
+GROUPS = PAST // 512
+
+F32 = mybir.dt.float32
+BF16 = mybir.dt.bfloat16
+U32 = mybir.dt.uint32
+I32 = mybir.dt.int32
+U8 = mybir.dt.uint8
+FP8 = mybir.dt.float8_e4m3fn
+FP8X4 = mybir.dt.float8_e4m3fn_x4
+FP4X4 = mybir.dt.float4_e2m1fn_x4
+ALU = mybir.AluOpType
+ACT = mybir.ActivationFunctionType
+
+
+def tile_reverb_prewhiten_replicas_s14_kernel(
+    tc, past_bytes, past_scale, now, taper, coef_words, coef_scales, bank_words, bank_scales, out
+):
+    nc = tc.nc
+    with ExitStack() as ctx:
+        keep = ctx.enter_context(tc.tile_pool(name="keep", bufs=1))
+        inp = ctx.enter_context(tc.tile_pool(name="inp", bufs=3))
+        work = ctx.enter_context(tc.tile_pool(name="work", bufs=3))
+        psum2 = ctx.enter_context(tc.psum_pool(name="psum2", bufs=2))
+        psum1 = ctx.enter_context(tc.psum_pool(name="psum1", bufs=1))
+
+        beams = {}
+
+        def load_past(b, split):
+            past_u8 = inp.tile([P, UNITS, PAST], U8, align_bytes=64)
+            src = past_bytes[b].rearrange("(r j) k -> r j k", j=UNITS)
+            if split:
+                for j in range(UNITS):
+                    nc.sync.dma_start(out=past_u8[:, j, :], in_=src[:, j, :])
+            else:
+                nc.sync.dma_start(out=past_u8[:], in_=src)
+            return past_u8
+
+        def load_now(b):
+            now_sb = inp.tile([P, UNITS, NOW], BF16, align_bytes=64)
+            nc.sync.dma_start(out=now_sb[:], in_=now[b].rearrange("(r j) n -> r j n", j=UNITS))
+            return now_sb
+
+        def load_coef(b):
+            coef = inp.tile([P, GROUPS, 2 * NOW], U8, align_bytes=64)
+            for g in range(GROUPS):
+                nc.sync.dma_start(
+                    out=coef[:, g, :].bitcast(I32), in_=coef_words[GROUPS * b + g].bitcast(I32)
+                )
+            return coef
+
+        def load_bank(b):
+            bank = inp.tile([P, 4 * DOPPLER], U8, align_bytes=64)
+            nc.sync.dma_start(out=bank[:].bitcast(I32), in_=bank_words[b].bitcast(I32))
+            return bank
+
+        coef_s = keep.tile([P, BEAMS * GROUPS, NOW], U8, align_bytes=64)
+        bank_s = keep.tile([P, BEAMS, 2 * DOPPLER], U8, align_bytes=64)
+        scale_sb = keep.tile([P, GROUPS, 4], F32, align_bytes=64)
+        taper_sb = keep.tile([P, BEAMS, 4], BF16, align_bytes=64)
+        ident = keep.tile([P, P], F32, align_bytes=64)
+        warm = keep.tile([P, 1], F32)
+
+        nc.vector.memset(coef_s[:].rearrange("p a n -> p (a n)").bitcast(I32), 0)
+        nc.gpsimd.memset(bank_s[:].rearrange("p a n -> p (a n)").bitcast(I32), 0)
+        make_identity(nc, ident[:])
+        nc.vector.memset(warm[:], 1.0)
+        nc.scalar.activation(out=warm[:], in_=warm[:], func=ACT.Sqrt)
+
+        past0 = load_past(0, True)
+        nc.sync.dma_start(out=scale_sb[:], in_=past_scale.rearrange("a b (g p t) -> p (a b g) t", p=P, t=4))
+        nc.sync.dma_start(out=taper_sb[:], in_=taper.rearrange("b (p t) -> p b t", t=4))
+        for q in range(4):
+            nc.sync.dma_start(
+                out=coef_s[32 * q : 32 * q + 4, :, :].bitcast(I32),
+                in_=coef_scales[:, 4 * q : 4 * q + 4, :].rearrange("a r n -> r a n").bitcast(I32),
+            )
+        coef0 = load_coef(0)
+        now0 = load_now(0)
+        for q in range(4):
+            nc.sync.dma_start(
+                out=bank_s[32 * q : 32 * q + 4, :, :].bitcast(I32),
+                in_=bank_scales[:, 4 * q : 4 * q + 4, :].rearrange("a r n -> r a n").bitcast(I32),
+            )
+        bank0 = load_bank(0)
+        beams[0] = (past0, now0, coef0, bank0)
+
+        def load_beam(b):
+            past_n = load_past(b, False)
+            coef_n = load_coef(b)
+            now_n = load_now(b)
+            bank_n = load_bank(b)
+            beams[b] = (past_n, now_n, coef_n, bank_n)
+
+        load_beam(1)
+
+        past16s, tps, groupeds, codes_p, preds, ds, dts, e16s, codes_e, ys, sqs, sums = (
+            {}, {}, {}, {}, {}, {}, {}, {}, {}, {}, {}, {}
+        )
+
+        def widen(i):
+            past_u8 = beams[i // UNITS][0]
+            past16 = work.tile([P, PAST], BF16, align_bytes=64)
+            nc.scalar.copy(out=past16[:], in_=past_u8[:, i % UNITS, :].bitcast(FP8))
+            past16s[i] = past16
+
+        def turn_past(i):
+            tp = psum2.tile([P, 512], F32)
+            words = past16s.pop(i)[:].bitcast(F32)
+            for u in range(2):
+                for g in range(GROUPS):
+                    col = u * 256 + g * P
+                    nc.tensor.transpose(
+                        tp[:, col : col + P], words[:, 256 * g + u : 256 * (g + 1) : 2], ident[:]
+                    )
+            tps[i] = tp
+
+        def scale_past(i):
+            grouped = work.tile([P, GROUPS, P, 4], BF16, align_bytes=64)
+            nc.vector.tensor_tensor(
+                out=grouped[:].rearrange("p g r t -> p (g r) t"),
+                in0=tps.pop(i)[:].bitcast(BF16).rearrange("p (u q e) -> p q u e", u=2, e=2),
+                in1=scale_sb[:].unsqueeze(2).to_broadcast([P, GROUPS, P, 4]),
+                op=ALU.mult,
+            )
+            groupeds[i] = grouped
+
+        def quant_past(i):
+            pc = work.tile([P, GROUPS, P], U32, align_bytes=64)
+            ps = work.tile([P, GROUPS, P], U8, align_bytes=64)
+            nc.vector.quantize_mx(
+                out=pc[:].rearrange("p g r -> p (g r)").bitcast(FP8X4),
+                scales=ps[:].rearrange("p g r -> p (g r)"),
+                in_=groupeds.pop(i)[:].rearrange("p g r t -> p (g r t)"),
+            )
+            codes_p[i] = (pc, ps)
+
+        def predict(i):
+            b = i // UNITS
+            coef = beams[b][2]
+            pc, ps = codes_p.pop(i)
+            pred = psum2.tile([P, NOW], F32)
+            for g in range(GROUPS):
+                nc.tensor.matmul_mx(
+                    out=pred[:],
+                    lhsT=pc[:, g, :].bitcast(FP8X4),
+                    lhsT_scale=ps[:, g, :],
+                    rhs=coef[:, g, :].bitcast(FP4X4),
+                    rhs_scale=coef_s[:, GROUPS * b + g, :],
+                    start=(g == 0),
+                    stop=(g == GROUPS - 1),
+                )
+            preds[i] = pred
+
+        def subtract(i):
+            d = work.tile([P, 4, P], F32, align_bytes=64)
+            nc.vector.tensor_tensor(
+                out=d[:],
+                in0=beams[i // UNITS][1][:, i % UNITS, :].rearrange("r (p t) -> r t p", t=4),
+                in1=preds.pop(i)[:].rearrange("r (p t) -> r t p", t=4),
+                op=ALU.subtract,
+            )
+            ds[i] = d
+
+        def turn_d(i):
+            dt = psum2.tile([P, 4, P], F32)
+            d = ds.pop(i)
+            for t in range(4):
+                nc.tensor.transpose(dt[:, t, :], d[:, t, :], ident[:])
+            dts[i] = dt
+
+        def apply_taper(i):
+            e16 = work.tile([P, P, 4], BF16, align_bytes=64)
+            nc.vector.tensor_tensor(
+                out=e16[:],
+                in0=dts.pop(i)[:].rearrange("p t r -> p r t"),
+                in1=taper_sb[:, i // UNITS, :].unsqueeze(1).to_broadcast([P, P, 4]),
+                op=ALU.mult,
+            )
+            e16s[i] = e16
+
+        def quant_e(i):
+            ec = work.tile([P, P], U32, align_bytes=64)
+            es = work.tile([P, P], U8, align_bytes=64)
+            nc.vector.quantize_mx(
+                out=ec[:].bitcast(FP8X4), scales=es[:], in_=e16s.pop(i)[:].rearrange("p r t -> p (r t)")
+            )
+            codes_e[i] = (ec, es)
+
+        def correlate(i):
+            b = i // UNITS
+            bank = beams[b][3]
+            ec, es = codes_e.pop(i)
+            y = psum1.tile([P, 2, DOPPLER], F32)
+            for h in range(2):
+                nc.tensor.matmul_mx(
+                    out=y[:, h, :],
+                    lhsT=ec[:].bitcast(FP8X4),
+                    lhsT_scale=es[:],
+                    rhs=bank[:, 2 * DOPPLER * h : 2 * DOPPLER * (h + 1)].bitcast(FP4X4),
+                    rhs_scale=bank_s[:, b, DOPPLER * h : DOPPLER * (h + 1)],
+                    start=True,
+                    stop=True,
+                )
+            ys[i] = y
+
+        def squares(i):
+            sq = work.tile([P, 2, DOPPLER], F32, align_bytes=64)
+            y = ys.pop(i)
+            for h in range(2):
+                nc.scalar.activation(out=sq[:, h, :], in_=y[:, h, :], func=ACT.Square)
+            sqs[i] = sq
+
+        def add(i):
+            power = work.tile([P, DOPPLER], F32, align_bytes=64)
+            sq = sqs.pop(i)
+            nc.gpsimd.tensor_tensor(out=power[:], in0=sq[:, 0, :], in1=sq[:, 1, :], op=ALU.add)
+            sums[i] = power
+
+        def root(i):
+            env = work.tile([P, DOPPLER], F32, align_bytes=64)
+            nc.scalar.activation(out=env[:], in_=sums.pop(i)[:], func=ACT.Sqrt)
+            nc.sync.dma_start(
+                out=out[i // UNITS].rearrange("(r j) d -> r j d", j=UNITS)[:, i % UNITS, :], in_=env[:]
+            )
+
+        with tc.manual_schedule():
+            for s in range(-2, STEPS + 6):
+                plan = (
+                    (quant_past, s - 1),
+                    (predict, s - 1),
+                    (subtract, s - 2),
+                    (turn_d, s - 2),
+                    (scale_past, s),
+                    (turn_past, s + 1),
+                    (apply_taper, s - 2),
+                    (quant_e, s - 3),
+                    (correlate, s - 3),
+                    (squares, s - 4),
+                    (add, s - 4),
+                    (widen, s + 2),
+                    (root, s - 5),
+                )
+                if s >= 0 and s % UNITS == 0 and s // UNITS + 2 < BEAMS:
+                    load_beam(s // UNITS + 2)
+                for stage, i in plan:
+                    if 0 <= i < STEPS:
+                        stage(i)

@@ -29,8 +29,8 @@ def tile_reverb_prewhiten_replicas_s14_kernel(
     nc = tc.nc
     with ExitStack() as ctx:
         keep = ctx.enter_context(tc.tile_pool(name="keep", bufs=1))
-        inp = ctx.enter_context(tc.tile_pool(name="inp", bufs=3))
-        work = ctx.enter_context(tc.tile_pool(name="work", bufs=3))
+        inp = ctx.enter_context(tc.tile_pool(name="inp", bufs=BEAMS))
+        work = ctx.enter_context(tc.tile_pool(name="work", bufs=4))
         psum2 = ctx.enter_context(tc.psum_pool(name="psum2", bufs=2))
         psum1 = ctx.enter_context(tc.psum_pool(name="psum1", bufs=1))
 
@@ -66,7 +66,7 @@ def tile_reverb_prewhiten_replicas_s14_kernel(
 
         coef_s = keep.tile([P, BEAMS * GROUPS, NOW], U8, align_bytes=64)
         bank_s = keep.tile([P, BEAMS, 2 * DOPPLER], U8, align_bytes=64)
-        scale_sb = keep.tile([P, GROUPS, 4], F32, align_bytes=64)
+        scale_sb = keep.tile([P, PAST], F32, align_bytes=64)
         taper_sb = keep.tile([P, BEAMS, 4], BF16, align_bytes=64)
         ident = keep.tile([P, P], F32, align_bytes=64)
         warm = keep.tile([P, 1], F32)
@@ -77,9 +77,13 @@ def tile_reverb_prewhiten_replicas_s14_kernel(
         nc.vector.memset(warm[:], 1.0)
         nc.scalar.activation(out=warm[:], in_=warm[:], func=ACT.Sqrt)
 
+        nc.sync.dma_start(out=scale_sb[:], in_=past_scale.rearrange("a b k -> (a b k)").partition_broadcast(P))
         past0 = load_past(0, True)
-        nc.sync.dma_start(out=scale_sb[:], in_=past_scale.rearrange("a b (g p t) -> p (a b g) t", p=P, t=4))
+        neg = keep.tile([P, P], BF16, align_bytes=64)
+        ntaper = keep.tile([P, BEAMS, 4], F32, align_bytes=64)
+        nc.vector.tensor_scalar(out=neg[:], in0=ident[:], scalar1=-1.0, scalar2=None, op0=ALU.mult)
         nc.sync.dma_start(out=taper_sb[:], in_=taper.rearrange("b (p t) -> p b t", t=4))
+        nc.vector.tensor_scalar(out=ntaper[:], in0=taper_sb[:], scalar1=-1.0, scalar2=None, op0=ALU.mult)
         for q in range(4):
             nc.sync.dma_start(
                 out=coef_s[32 * q : 32 * q + 4, :, :].bitcast(I32),
@@ -103,6 +107,7 @@ def tile_reverb_prewhiten_replicas_s14_kernel(
             beams[b] = (past_n, now_n, coef_n, bank_n)
 
         load_beam(1)
+        load_beam(2)
 
         past16s, tps, groupeds, codes_p, preds, ds, dts, e16s, codes_e, ys, sqs, sums = (
             {}, {}, {}, {}, {}, {}, {}, {}, {}, {}, {}, {}
@@ -111,7 +116,9 @@ def tile_reverb_prewhiten_replicas_s14_kernel(
         def widen(i):
             past_u8 = beams[i // UNITS][0]
             past16 = work.tile([P, PAST], BF16, align_bytes=64)
-            nc.scalar.copy(out=past16[:], in_=past_u8[:, i % UNITS, :].bitcast(FP8))
+            nc.vector.tensor_tensor(
+                out=past16[:], in0=past_u8[:, i % UNITS, :].bitcast(FP8), in1=scale_sb[:], op=ALU.mult
+            )
             past16s[i] = past16
 
         def turn_past(i):
@@ -127,11 +134,9 @@ def tile_reverb_prewhiten_replicas_s14_kernel(
 
         def scale_past(i):
             grouped = work.tile([P, GROUPS, P, 4], BF16, align_bytes=64)
-            nc.vector.tensor_tensor(
-                out=grouped[:].rearrange("p g r t -> p (g r) t"),
-                in0=tps.pop(i)[:].bitcast(BF16).rearrange("p (u q e) -> p q u e", u=2, e=2),
-                in1=scale_sb[:].unsqueeze(2).to_broadcast([P, GROUPS, P, 4]),
-                op=ALU.mult,
+            nc.scalar.copy(
+                out=grouped[:].rearrange("p g r t -> p (g r t)").bitcast(F32).rearrange("p (q u) -> p q u", u=2),
+                in_=tps.pop(i)[:].rearrange("p (u q) -> p q u", u=2),
             )
             groupeds[i] = grouped
 
@@ -164,19 +169,19 @@ def tile_reverb_prewhiten_replicas_s14_kernel(
 
         def subtract(i):
             d = work.tile([P, 4, P], F32, align_bytes=64)
-            nc.vector.tensor_tensor(
-                out=d[:],
-                in0=beams[i // UNITS][1][:, i % UNITS, :].rearrange("r (p t) -> r t p", t=4),
-                in1=preds.pop(i)[:].rearrange("r (p t) -> r t p", t=4),
-                op=ALU.subtract,
-            )
+            nc.scalar.copy(out=d[:], in_=preds.pop(i)[:].rearrange("r (p t) -> r t p", t=4))
             ds[i] = d
 
         def turn_d(i):
             dt = psum2.tile([P, 4, P], F32)
             d = ds.pop(i)
+            now_u = beams[i // UNITS][1][:, i % UNITS, :]
             for t in range(4):
-                nc.tensor.transpose(dt[:, t, :], d[:, t, :], ident[:])
+                nc.tensor.matmul(dt[:, t, :], lhsT=now_u[:, t::4], rhs=neg[:], start=(t == 0), stop=False)
+            for t in range(4):
+                nc.tensor.matmul(
+                    dt[:, t, :], lhsT=d[:, t, :], rhs=ident[:], is_transpose=True, start=False, stop=(t == 3)
+                )
             dts[i] = dt
 
         def apply_taper(i):
@@ -184,7 +189,7 @@ def tile_reverb_prewhiten_replicas_s14_kernel(
             nc.vector.tensor_tensor(
                 out=e16[:],
                 in0=dts.pop(i)[:].rearrange("p t r -> p r t"),
-                in1=taper_sb[:, i // UNITS, :].unsqueeze(1).to_broadcast([P, P, 4]),
+                in1=ntaper[:, i // UNITS, :].unsqueeze(1).to_broadcast([P, P, 4]),
                 op=ALU.mult,
             )
             e16s[i] = e16
@@ -201,10 +206,11 @@ def tile_reverb_prewhiten_replicas_s14_kernel(
             b = i // UNITS
             bank = beams[b][3]
             ec, es = codes_e.pop(i)
-            y = psum1.tile([P, 2, DOPPLER], F32)
-            for h in range(2):
+            y_i = psum1.tile([P, DOPPLER], F32)
+            y_q = psum1.tile([P, DOPPLER], F32)
+            for h, y in enumerate((y_i, y_q)):
                 nc.tensor.matmul_mx(
-                    out=y[:, h, :],
+                    out=y[:],
                     lhsT=ec[:].bitcast(FP8X4),
                     lhsT_scale=es[:],
                     rhs=bank[:, 2 * DOPPLER * h : 2 * DOPPLER * (h + 1)].bitcast(FP4X4),
@@ -212,19 +218,20 @@ def tile_reverb_prewhiten_replicas_s14_kernel(
                     start=True,
                     stop=True,
                 )
-            ys[i] = y
+            ys[i] = (y_i, y_q)
 
-        def squares(i):
+        def square_i(i):
             sq = work.tile([P, 2, DOPPLER], F32, align_bytes=64)
-            y = ys.pop(i)
-            for h in range(2):
-                nc.scalar.activation(out=sq[:, h, :], in_=y[:, h, :], func=ACT.Square)
+            nc.scalar.activation(out=sq[:, 0, :], in_=ys[i][0][:], func=ACT.Square)
             sqs[i] = sq
+
+        def square_q(i):
+            nc.scalar.activation(out=sqs[i][:, 1, :], in_=ys.pop(i)[1][:], func=ACT.Square)
 
         def add(i):
             power = work.tile([P, DOPPLER], F32, align_bytes=64)
             sq = sqs.pop(i)
-            nc.gpsimd.tensor_tensor(out=power[:], in0=sq[:, 0, :], in1=sq[:, 1, :], op=ALU.add)
+            nc.vector.tensor_tensor(out=power[:], in0=sq[:, 0, :], in1=sq[:, 1, :], op=ALU.add)
             sums[i] = power
 
         def root(i):
@@ -235,24 +242,25 @@ def tile_reverb_prewhiten_replicas_s14_kernel(
             )
 
         with tc.manual_schedule():
-            for s in range(-2, STEPS + 6):
+            for s in range(STEPS + 8):
                 plan = (
-                    (quant_past, s - 1),
-                    (predict, s - 1),
-                    (subtract, s - 2),
-                    (turn_d, s - 2),
-                    (scale_past, s),
-                    (turn_past, s + 1),
-                    (apply_taper, s - 2),
-                    (quant_e, s - 3),
-                    (correlate, s - 3),
-                    (squares, s - 4),
-                    (add, s - 4),
-                    (widen, s + 2),
-                    (root, s - 5),
+                    (widen, s),
+                    (scale_past, s - 1),
+                    (turn_past, s),
+                    (apply_taper, s - 5),
+                    (subtract, s - 4),
+                    (root, s - 8),
+                    (quant_past, s - 2),
+                    (square_i, s - 6),
+                    (predict, s - 3),
+                    (turn_d, s - 4),
+                    (square_q, s - 6),
+                    (add, s - 7),
+                    (quant_e, s - 5),
+                    (correlate, s - 5),
                 )
-                if s >= 0 and s % UNITS == 0 and s // UNITS + 2 < BEAMS:
-                    load_beam(s // UNITS + 2)
+                if s % UNITS == 0 and s // UNITS + 3 < BEAMS:
+                    load_beam(s // UNITS + 3)
                 for stage, i in plan:
                     if 0 <= i < STEPS:
                         stage(i)

@@ -35,6 +35,7 @@ def tile_reverb_prewhiten_replicas_s14_kernel(
         psum1 = ctx.enter_context(tc.psum_pool(name="psum1", bufs=1))
 
         beams = {}
+        on_vector = range(STEPS - 4, STEPS)
 
         def load_past(b, split):
             past_u8 = inp.tile([P, UNITS, PAST], U8, align_bytes=64)
@@ -77,7 +78,7 @@ def tile_reverb_prewhiten_replicas_s14_kernel(
         nc.vector.memset(warm[:], 1.0)
         nc.scalar.activation(out=warm[:], in_=warm[:], func=ACT.Sqrt)
 
-        nc.sync.dma_start(out=scale_sb[:], in_=past_scale.rearrange("a b k -> (a b k)").partition_broadcast(P))
+        nc.scalar.dma_start(out=scale_sb[:], in_=past_scale.rearrange("a b k -> (a b k)").partition_broadcast(P))
         past0 = load_past(0, True)
         neg = keep.tile([P, P], BF16, align_bytes=64)
         ntaper = keep.tile([P, BEAMS, 4], F32, align_bytes=64)
@@ -169,19 +170,30 @@ def tile_reverb_prewhiten_replicas_s14_kernel(
 
         def subtract(i):
             d = work.tile([P, 4, P], F32, align_bytes=64)
-            nc.scalar.copy(out=d[:], in_=preds.pop(i)[:].rearrange("r (p t) -> r t p", t=4))
+            pred = preds.pop(i)[:].rearrange("r (p t) -> r t p", t=4)
+            if i in on_vector:
+                nc.vector.tensor_tensor(
+                    out=d[:], in0=pred, in1=beams[i // UNITS][1][:, i % UNITS, :].rearrange("r (p t) -> r t p", t=4),
+                    op=ALU.subtract,
+                )
+            else:
+                nc.scalar.copy(out=d[:], in_=pred)
             ds[i] = d
 
         def turn_d(i):
             dt = psum2.tile([P, 4, P], F32)
             d = ds.pop(i)
             now_u = beams[i // UNITS][1][:, i % UNITS, :]
-            for t in range(4):
-                nc.tensor.matmul(dt[:, t, :], lhsT=now_u[:, t::4], rhs=neg[:], start=(t == 0), stop=False)
-            for t in range(4):
-                nc.tensor.matmul(
-                    dt[:, t, :], lhsT=d[:, t, :], rhs=ident[:], is_transpose=True, start=False, stop=(t == 3)
-                )
+            if i in on_vector:
+                for t in range(4):
+                    nc.tensor.transpose(dt[:, t, :], d[:, t, :], ident[:])
+            else:
+                for t in range(4):
+                    nc.tensor.matmul(dt[:, t, :], lhsT=now_u[:, t::4], rhs=neg[:], start=(t == 0), stop=False)
+                for t in range(4):
+                    nc.tensor.matmul(
+                        dt[:, t, :], lhsT=d[:, t, :], rhs=ident[:], is_transpose=True, start=False, stop=(t == 3)
+                    )
             dts[i] = dt
 
         def apply_taper(i):
@@ -244,19 +256,19 @@ def tile_reverb_prewhiten_replicas_s14_kernel(
         with tc.manual_schedule():
             for s in range(STEPS + 8):
                 plan = (
-                    (widen, s),
-                    (scale_past, s - 1),
-                    (turn_past, s),
-                    (apply_taper, s - 5),
                     (subtract, s - 4),
-                    (root, s - 8),
-                    (quant_past, s - 2),
-                    (square_i, s - 6),
                     (predict, s - 3),
-                    (turn_d, s - 4),
-                    (square_q, s - 6),
+                    (root, s - 8),
+                    (scale_past, s - 1),
+                    (square_i, s - 6),
+                    (widen, s),
+                    (quant_past, s - 2),
+                    (apply_taper, s - 5),
                     (add, s - 7),
+                    (turn_past, s),
                     (quant_e, s - 5),
+                    (square_q, s - 6),
+                    (turn_d, s - 4),
                     (correlate, s - 5),
                 )
                 if s % UNITS == 0 and s // UNITS + 3 < BEAMS:

@@ -79,12 +79,17 @@ def tile_reverb_prewhiten_replicas_s14_kernel(
         nc.scalar.activation(out=warm[:], in_=warm[:], func=ACT.Sqrt)
 
         nc.scalar.dma_start(out=scale_sb[:], in_=past_scale.rearrange("a b k -> (a b k)").partition_broadcast(P))
-        past0 = load_past(0, True)
-        neg = keep.tile([P, P], BF16, align_bytes=64)
-        ntaper = keep.tile([P, BEAMS, 4], F32, align_bytes=64)
-        nc.vector.tensor_scalar(out=neg[:], in0=ident[:], scalar1=-1.0, scalar2=None, op0=ALU.mult)
+        ident16 = keep.tile([P, P], BF16, align_bytes=64)
+        nc.vector.tensor_copy(out=ident16[:], in_=ident[:])
         nc.sync.dma_start(out=taper_sb[:], in_=taper.rearrange("b (p t) -> p b t", t=4))
-        nc.vector.tensor_scalar(out=ntaper[:], in0=taper_sb[:], scalar1=-1.0, scalar2=None, op0=ALU.mult)
+        past0 = load_past(0, True)
+        taper_x = keep.tile([P, BEAMS, P, 4], BF16, align_bytes=64)
+        for b0 in (0, BEAMS // 2):
+            half = slice(b0, b0 + BEAMS // 2)
+            nc.scalar.copy(
+                out=taper_x[:, half, :, :],
+                in_=taper_sb[:, half, :].unsqueeze(2).to_broadcast([P, BEAMS // 2, P, 4]),
+            )
         for q in range(4):
             nc.sync.dma_start(
                 out=coef_s[32 * q : 32 * q + 4, :, :].bitcast(I32),
@@ -173,11 +178,11 @@ def tile_reverb_prewhiten_replicas_s14_kernel(
             pred = preds.pop(i)[:].rearrange("r (p t) -> r t p", t=4)
             if i in on_vector:
                 nc.vector.tensor_tensor(
-                    out=d[:], in0=pred, in1=beams[i // UNITS][1][:, i % UNITS, :].rearrange("r (p t) -> r t p", t=4),
+                    out=d[:], in0=beams[i // UNITS][1][:, i % UNITS, :].rearrange("r (p t) -> r t p", t=4), in1=pred,
                     op=ALU.subtract,
                 )
             else:
-                nc.scalar.copy(out=d[:], in_=pred)
+                nc.scalar.activation(out=d[:], in_=pred, func=ACT.Copy, scale=-1.0)
             ds[i] = d
 
         def turn_d(i):
@@ -189,7 +194,7 @@ def tile_reverb_prewhiten_replicas_s14_kernel(
                     nc.tensor.transpose(dt[:, t, :], d[:, t, :], ident[:])
             else:
                 for t in range(4):
-                    nc.tensor.matmul(dt[:, t, :], lhsT=now_u[:, t::4], rhs=neg[:], start=(t == 0), stop=False)
+                    nc.tensor.matmul(dt[:, t, :], lhsT=now_u[:, t::4], rhs=ident16[:], start=(t == 0), stop=False)
                 for t in range(4):
                     nc.tensor.matmul(
                         dt[:, t, :], lhsT=d[:, t, :], rhs=ident[:], is_transpose=True, start=False, stop=(t == 3)
@@ -201,7 +206,7 @@ def tile_reverb_prewhiten_replicas_s14_kernel(
             nc.vector.tensor_tensor(
                 out=e16[:],
                 in0=dts.pop(i)[:].rearrange("p t r -> p r t"),
-                in1=ntaper[:, i // UNITS, :].unsqueeze(1).to_broadcast([P, P, 4]),
+                in1=taper_x[:, i // UNITS, :, :],
                 op=ALU.mult,
             )
             e16s[i] = e16

@@ -29,8 +29,9 @@ def tile_reverb_prewhiten_replicas_s14_kernel(
     nc = tc.nc
     with ExitStack() as ctx:
         keep = ctx.enter_context(tc.tile_pool(name="keep", bufs=1))
-        inp = ctx.enter_context(tc.tile_pool(name="inp", bufs=BEAMS))
-        work = ctx.enter_context(tc.tile_pool(name="work", bufs=4))
+        inp = ctx.enter_context(tc.tile_pool(name="inp", bufs=6))
+        work = ctx.enter_context(tc.tile_pool(name="work", bufs=3))
+        outs = ctx.enter_context(tc.tile_pool(name="outs", bufs=STEPS))
         psum2 = ctx.enter_context(tc.psum_pool(name="psum2", bufs=2))
         psum1 = ctx.enter_context(tc.psum_pool(name="psum1", bufs=1))
 
@@ -54,10 +55,10 @@ def tile_reverb_prewhiten_replicas_s14_kernel(
 
         def load_coef(b):
             coef = inp.tile([P, GROUPS, 2 * NOW], U8, align_bytes=64)
-            for g in range(GROUPS):
-                nc.sync.dma_start(
-                    out=coef[:, g, :].bitcast(I32), in_=coef_words[GROUPS * b + g].bitcast(I32)
-                )
+            nc.sync.dma_start(
+                out=coef[:].bitcast(I32),
+                in_=coef_words[GROUPS * b : GROUPS * (b + 1)].rearrange("g p n -> p g n").bitcast(I32),
+            )
             return coef
 
         def load_bank(b):
@@ -72,24 +73,17 @@ def tile_reverb_prewhiten_replicas_s14_kernel(
         ident = keep.tile([P, P], F32, align_bytes=64)
         warm = keep.tile([P, 1], F32)
 
-        nc.vector.memset(coef_s[:].rearrange("p a n -> p (a n)").bitcast(I32), 0)
-        nc.gpsimd.memset(bank_s[:].rearrange("p a n -> p (a n)").bitcast(I32), 0)
-        make_identity(nc, ident[:])
-        nc.vector.memset(warm[:], 1.0)
-        nc.scalar.activation(out=warm[:], in_=warm[:], func=ACT.Sqrt)
-
-        nc.scalar.dma_start(out=scale_sb[:], in_=past_scale.rearrange("a b k -> (a b k)").partition_broadcast(P))
         ident16 = keep.tile([P, P], BF16, align_bytes=64)
-        nc.vector.tensor_copy(out=ident16[:], in_=ident[:])
-        nc.sync.dma_start(out=taper_sb[:], in_=taper.rearrange("b (p t) -> p b t", t=4))
-        past0 = load_past(0, True)
         taper_x = keep.tile([P, BEAMS, P, 4], BF16, align_bytes=64)
-        for b0 in (0, BEAMS // 2):
-            half = slice(b0, b0 + BEAMS // 2)
-            nc.scalar.copy(
-                out=taper_x[:, half, :, :],
-                in_=taper_sb[:, half, :].unsqueeze(2).to_broadcast([P, BEAMS // 2, P, 4]),
-            )
+
+        nc.sync.dma_start(out=scale_sb[:], in_=past_scale.rearrange("a b k -> (a b k)").partition_broadcast(P))
+        past0 = load_past(0, True)
+        nc.vector.memset(warm[:], 1.0)
+        nc.vector.memset(coef_s[:].rearrange("p a n -> p (a n)").bitcast(I32), 0)
+        make_identity(nc, ident[:])
+        nc.gpsimd.memset(bank_s[:].rearrange("p a n -> p (a n)").bitcast(I32), 0)
+        nc.scalar.activation(out=warm[:], in_=warm[:], func=ACT.Sqrt)
+        nc.scalar.copy(out=ident16[:], in_=ident[:])
         for q in range(4):
             nc.sync.dma_start(
                 out=coef_s[32 * q : 32 * q + 4, :, :].bitcast(I32),
@@ -97,6 +91,7 @@ def tile_reverb_prewhiten_replicas_s14_kernel(
             )
         coef0 = load_coef(0)
         now0 = load_now(0)
+        nc.sync.dma_start(out=taper_sb[:], in_=taper.rearrange("b (p t) -> p b t", t=4))
         for q in range(4):
             nc.sync.dma_start(
                 out=bank_s[32 * q : 32 * q + 4, :, :].bitcast(I32),
@@ -118,6 +113,12 @@ def tile_reverb_prewhiten_replicas_s14_kernel(
         past16s, tps, groupeds, codes_p, preds, ds, dts, e16s, codes_e, ys, sqs, sums = (
             {}, {}, {}, {}, {}, {}, {}, {}, {}, {}, {}, {}
         )
+
+        def spread_taper(b):
+            nc.scalar.copy(
+                out=taper_x[:, b : b + 2, :, :].bitcast(F32),
+                in_=taper_sb[:, b : b + 2, :].bitcast(F32).unsqueeze(2).to_broadcast([P, 2, P, 2]),
+            )
 
         def widen(i):
             past_u8 = beams[i // UNITS][0]
@@ -252,32 +253,34 @@ def tile_reverb_prewhiten_replicas_s14_kernel(
             sums[i] = power
 
         def root(i):
-            env = work.tile([P, DOPPLER], F32, align_bytes=64)
+            env = outs.tile([P, DOPPLER], F32, align_bytes=64)
             nc.scalar.activation(out=env[:], in_=sums.pop(i)[:], func=ACT.Sqrt)
             nc.sync.dma_start(
                 out=out[i // UNITS].rearrange("(r j) d -> r j d", j=UNITS)[:, i % UNITS, :], in_=env[:]
             )
 
         with tc.manual_schedule():
-            for s in range(STEPS + 8):
+            for s in range(STEPS + 9):
                 plan = (
+                    (widen, s),
                     (subtract, s - 4),
                     (predict, s - 3),
-                    (root, s - 8),
-                    (scale_past, s - 1),
-                    (square_i, s - 6),
-                    (widen, s),
-                    (quant_past, s - 2),
                     (apply_taper, s - 5),
-                    (add, s - 7),
-                    (turn_past, s),
-                    (quant_e, s - 5),
-                    (square_q, s - 6),
+                    (root, s - 9),
+                    (correlate, s - 6),
+                    (add, s - 8),
+                    (scale_past, s - 1),
                     (turn_d, s - 4),
-                    (correlate, s - 5),
+                    (quant_e, s - 5),
+                    (quant_past, s - 2),
+                    (square_i, s - 6),
+                    (square_q, s - 6),
+                    (turn_past, s),
                 )
                 if s % UNITS == 0 and s // UNITS + 3 < BEAMS:
                     load_beam(s // UNITS + 3)
                 for stage, i in plan:
                     if 0 <= i < STEPS:
                         stage(i)
+                if 3 <= s < 3 + BEAMS // 2:
+                    spread_taper(2 * (s - 3))

from contextlib import ExitStack

import concourse.mybir as mybir
from concourse.masks import make_identity

BEAMS, PINGS, PAST, NOW, DOPPLER = 8, 512, 1024, 512, 512
FLOPS = 2 * BEAMS * PINGS * (PAST * NOW + NOW * 2 * DOPPLER)

P = 128
UNITS = PINGS // P
STEPS = BEAMS * UNITS
GROUPS = PAST // 512

F32 = mybir.dt.float32
BF16 = mybir.dt.bfloat16
U32 = mybir.dt.uint32
I32 = mybir.dt.int32
U8 = mybir.dt.uint8
FP8 = mybir.dt.float8_e4m3fn
FP8X4 = mybir.dt.float8_e4m3fn_x4
FP4X4 = mybir.dt.float4_e2m1fn_x4
ALU = mybir.AluOpType
ACT = mybir.ActivationFunctionType


def tile_reverb_prewhiten_replicas_s14_kernel(
    tc, past_bytes, past_scale, now, taper, coef_words, coef_scales, bank_words, bank_scales, out
):
    nc = tc.nc
    with ExitStack() as ctx:
        keep = ctx.enter_context(tc.tile_pool(name="keep", bufs=1))
        inp = ctx.enter_context(tc.tile_pool(name="inp", bufs=6))
        work = ctx.enter_context(tc.tile_pool(name="work", bufs=3))
        outs = ctx.enter_context(tc.tile_pool(name="outs", bufs=STEPS))
        psum2 = ctx.enter_context(tc.psum_pool(name="psum2", bufs=2))
        psum1 = ctx.enter_context(tc.psum_pool(name="psum1", bufs=1))

        beams = {}
        on_vector = range(STEPS - 4, STEPS)

        def load_past(b, split):
            past_u8 = inp.tile([P, UNITS, PAST], U8, align_bytes=64)
            src = past_bytes[b].rearrange("(r j) k -> r j k", j=UNITS)
            if split:
                for j in range(UNITS):
                    nc.sync.dma_start(out=past_u8[:, j, :], in_=src[:, j, :])
            else:
                nc.sync.dma_start(out=past_u8[:], in_=src)
            return past_u8

        def load_now(b):
            now_sb = inp.tile([P, UNITS, NOW], BF16, align_bytes=64)
            nc.sync.dma_start(out=now_sb[:], in_=now[b].rearrange("(r j) n -> r j n", j=UNITS))
            return now_sb

        def load_coef(b):
            coef = inp.tile([P, GROUPS, 2 * NOW], U8, align_bytes=64)
            nc.sync.dma_start(
                out=coef[:].bitcast(I32),
                in_=coef_words[GROUPS * b : GROUPS * (b + 1)].rearrange("g p n -> p g n").bitcast(I32),
            )
            return coef

        def load_bank(b):
            bank = inp.tile([P, 4 * DOPPLER], U8, align_bytes=64)
            nc.sync.dma_start(out=bank[:].bitcast(I32), in_=bank_words[b].bitcast(I32))
            return bank

        coef_s = keep.tile([P, BEAMS * GROUPS, NOW], U8, align_bytes=64)
        bank_s = keep.tile([P, BEAMS, 2 * DOPPLER], U8, align_bytes=64)
        scale_sb = keep.tile([P, PAST], F32, align_bytes=64)
        taper_sb = keep.tile([P, BEAMS, 4], BF16, align_bytes=64)
        ident = keep.tile([P, P], F32, align_bytes=64)
        warm = keep.tile([P, 1], F32)

        ident16 = keep.tile([P, P], BF16, align_bytes=64)
        taper_x = keep.tile([P, BEAMS, P, 4], BF16, align_bytes=64)

        nc.sync.dma_start(out=scale_sb[:], in_=past_scale.rearrange("a b k -> (a b k)").partition_broadcast(P))
        past0 = load_past(0, True)
        nc.vector.memset(warm[:], 1.0)
        nc.vector.memset(coef_s[:].rearrange("p a n -> p (a n)").bitcast(I32), 0)
        make_identity(nc, ident[:])
        nc.gpsimd.memset(bank_s[:].rearrange("p a n -> p (a n)").bitcast(I32), 0)
        nc.scalar.activation(out=warm[:], in_=warm[:], func=ACT.Sqrt)
        nc.scalar.copy(out=ident16[:], in_=ident[:])
        for q in range(4):
            nc.sync.dma_start(
                out=coef_s[32 * q : 32 * q + 4, :, :].bitcast(I32),
                in_=coef_scales[:, 4 * q : 4 * q + 4, :].rearrange("a r n -> r a n").bitcast(I32),
            )
        coef0 = load_coef(0)
        now0 = load_now(0)
        nc.sync.dma_start(out=taper_sb[:], in_=taper.rearrange("b (p t) -> p b t", t=4))
        for q in range(4):
            nc.sync.dma_start(
                out=bank_s[32 * q : 32 * q + 4, :, :].bitcast(I32),
                in_=bank_scales[:, 4 * q : 4 * q + 4, :].rearrange("a r n -> r a n").bitcast(I32),
            )
        bank0 = load_bank(0)
        beams[0] = (past0, now0, coef0, bank0)

        def load_beam(b):
            past_n = load_past(b, False)
            coef_n = load_coef(b)
            now_n = load_now(b)
            bank_n = load_bank(b)
            beams[b] = (past_n, now_n, coef_n, bank_n)

        load_beam(1)
        load_beam(2)

        past16s, tps, groupeds, codes_p, preds, ds, dts, e16s, codes_e, ys, sqs, sums = (
            {}, {}, {}, {}, {}, {}, {}, {}, {}, {}, {}, {}
        )

        def spread_taper(b):
            nc.scalar.copy(
                out=taper_x[:, b : b + 2, :, :].bitcast(F32),
                in_=taper_sb[:, b : b + 2, :].bitcast(F32).unsqueeze(2).to_broadcast([P, 2, P, 2]),
            )

        def widen(i):
            past_u8 = beams[i // UNITS][0]
            past16 = work.tile([P, PAST], BF16, align_bytes=64)
            nc.vector.tensor_tensor(
                out=past16[:], in0=past_u8[:, i % UNITS, :].bitcast(FP8), in1=scale_sb[:], op=ALU.mult
            )
            past16s[i] = past16

        def turn_past(i):
            tp = psum2.tile([P, 512], F32)
            words = past16s.pop(i)[:].bitcast(F32)
            for u in range(2):
                for g in range(GROUPS):
                    col = u * 256 + g * P
                    nc.tensor.transpose(
                        tp[:, col : col + P], words[:, 256 * g + u : 256 * (g + 1) : 2], ident[:]
                    )
            tps[i] = tp

        def scale_past(i):
            grouped = work.tile([P, GROUPS, P, 4], BF16, align_bytes=64)
            nc.scalar.copy(
                out=grouped[:].rearrange("p g r t -> p (g r t)").bitcast(F32).rearrange("p (q u) -> p q u", u=2),
                in_=tps.pop(i)[:].rearrange("p (u q) -> p q u", u=2),
            )
            groupeds[i] = grouped

        def quant_past(i):
            pc = work.tile([P, GROUPS, P], U32, align_bytes=64)
            ps = work.tile([P, GROUPS, P], U8, align_bytes=64)
            nc.vector.quantize_mx(
                out=pc[:].rearrange("p g r -> p (g r)").bitcast(FP8X4),
                scales=ps[:].rearrange("p g r -> p (g r)"),
                in_=groupeds.pop(i)[:].rearrange("p g r t -> p (g r t)"),
            )
            codes_p[i] = (pc, ps)

        def predict(i):
            b = i // UNITS
            coef = beams[b][2]
            pc, ps = codes_p.pop(i)
            pred = psum2.tile([P, NOW], F32)
            for g in range(GROUPS):
                nc.tensor.matmul_mx(
                    out=pred[:],
                    lhsT=pc[:, g, :].bitcast(FP8X4),
                    lhsT_scale=ps[:, g, :],
                    rhs=coef[:, g, :].bitcast(FP4X4),
                    rhs_scale=coef_s[:, GROUPS * b + g, :],
                    start=(g == 0),
                    stop=(g == GROUPS - 1),
                )
            preds[i] = pred

        def subtract(i):
            d = work.tile([P, 4, P], F32, align_bytes=64)
            pred = preds.pop(i)[:].rearrange("r (p t) -> r t p", t=4)
            if i in on_vector:
                nc.vector.tensor_tensor(
                    out=d[:], in0=beams[i // UNITS][1][:, i % UNITS, :].rearrange("r (p t) -> r t p", t=4), in1=pred,
                    op=ALU.subtract,
                )
            else:
                nc.scalar.activation(out=d[:], in_=pred, func=ACT.Copy, scale=-1.0)
            ds[i] = d

        def turn_d(i):
            dt = psum2.tile([P, 4, P], F32)
            d = ds.pop(i)
            now_u = beams[i // UNITS][1][:, i % UNITS, :]
            if i in on_vector:
                for t in range(4):
                    nc.tensor.transpose(dt[:, t, :], d[:, t, :], ident[:])
            else:
                for t in range(4):
                    nc.tensor.matmul(dt[:, t, :], lhsT=now_u[:, t::4], rhs=ident16[:], start=(t == 0), stop=False)
                for t in range(4):
                    nc.tensor.matmul(
                        dt[:, t, :], lhsT=d[:, t, :], rhs=ident[:], is_transpose=True, start=False, stop=(t == 3)
                    )
            dts[i] = dt

        def apply_taper(i):
            e16 = work.tile([P, P, 4], BF16, align_bytes=64)
            nc.vector.tensor_tensor(
                out=e16[:],
                in0=dts.pop(i)[:].rearrange("p t r -> p r t"),
                in1=taper_x[:, i // UNITS, :, :],
                op=ALU.mult,
            )
            e16s[i] = e16

        def quant_e(i):
            ec = work.tile([P, P], U32, align_bytes=64)
            es = work.tile([P, P], U8, align_bytes=64)
            nc.vector.quantize_mx(
                out=ec[:].bitcast(FP8X4), scales=es[:], in_=e16s.pop(i)[:].rearrange("p r t -> p (r t)")
            )
            codes_e[i] = (ec, es)

        def correlate(i):
            b = i // UNITS
            bank = beams[b][3]
            ec, es = codes_e.pop(i)
            y_i = psum1.tile([P, DOPPLER], F32)
            y_q = psum1.tile([P, DOPPLER], F32)
            for h, y in enumerate((y_i, y_q)):
                nc.tensor.matmul_mx(
                    out=y[:],
                    lhsT=ec[:].bitcast(FP8X4),
                    lhsT_scale=es[:],
                    rhs=bank[:, 2 * DOPPLER * h : 2 * DOPPLER * (h + 1)].bitcast(FP4X4),
                    rhs_scale=bank_s[:, b, DOPPLER * h : DOPPLER * (h + 1)],
                    start=True,
                    stop=True,
                )
            ys[i] = (y_i, y_q)

        def square_i(i):
            sq = work.tile([P, 2, DOPPLER], F32, align_bytes=64)
            nc.scalar.activation(out=sq[:, 0, :], in_=ys[i][0][:], func=ACT.Square)
            sqs[i] = sq

        def square_q(i):
            nc.scalar.activation(out=sqs[i][:, 1, :], in_=ys.pop(i)[1][:], func=ACT.Square)

        def add(i):
            power = work.tile([P, DOPPLER], F32, align_bytes=64)
            sq = sqs.pop(i)
            nc.vector.tensor_tensor(out=power[:], in0=sq[:, 0, :], in1=sq[:, 1, :], op=ALU.add)
            sums[i] = power

        def root(i):
            env = outs.tile([P, DOPPLER], F32, align_bytes=64)
            nc.scalar.activation(out=env[:], in_=sums.pop(i)[:], func=ACT.Sqrt)
            nc.sync.dma_start(
                out=out[i // UNITS].rearrange("(r j) d -> r j d", j=UNITS)[:, i % UNITS, :], in_=env[:]
            )

        with tc.manual_schedule():
            for s in range(STEPS + 9):
                plan = (
                    (widen, s),
                    (subtract, s - 4),
                    (predict, s - 3),
                    (apply_taper, s - 5),
                    (root, s - 9),
                    (correlate, s - 6),
                    (add, s - 8),
                    (scale_past, s - 1),
                    (turn_d, s - 4),
                    (quant_e, s - 5),
                    (quant_past, s - 2),
                    (square_i, s - 6),
                    (square_q, s - 6),
                    (turn_past, s),
                )
                if s % UNITS == 0 and s // UNITS + 3 < BEAMS:
                    load_beam(s // UNITS + 3)
                for stage, i in plan:
                    if 0 <= i < STEPS:
                        stage(i)
                if 3 <= s < 3 + BEAMS // 2:
                    spread_taper(2 * (s - 3))
